import numpy as np
import ml_dtypes


def mxq(x, axis, fmt="e4m3"):
    dtype, down = {"e4m3": (ml_dtypes.float8_e4m3fn, 7), "e5m2": (ml_dtypes.float8_e5m2, 14)}[fmt]
    v = np.moveaxis(np.asarray(x, np.float32).astype(ml_dtypes.bfloat16).astype(np.float64), axis, -1)
    blocks = v.reshape(v.shape[:-1] + (-1, 32))
    amax = np.abs(blocks).max(-1, keepdims=True)
    byte = np.maximum(np.where(amax > 0, np.frexp(amax)[1] - 1 + 127, 0) - down, 1)
    scale = np.exp2(byte - 127.0)
    codes = (blocks / scale).astype(np.float32).astype(dtype).astype(np.float64)
    return np.moveaxis((codes * scale).reshape(v.shape), -1, axis)


WIDE = False


def mx_kscale(k):
    if not WIDE:
        return np.ones(k)
    levels = np.array([10, -10, 5, -5, 0])
    if k % 512:
        return np.exp2(np.random.permutation(np.resize(levels, k // 32))).repeat(32)
    a = np.empty((k // 512, 16))
    for p in range(k // 512):
        a[p, :8] = np.random.permutation(np.resize(levels, 8))
        for g in range(8):
            far = levels[np.abs(levels - a[p, g]) >= 10]
            a[p, g + 8] = far[np.random.randint(len(far))]
    return np.exp2(a.ravel()).repeat(32)


def f64(x):
    return np.asarray(x).astype(np.float64)


def striped(idx):
    return np.tile(idx.reshape(-1, 16).T, (8, 1)).astype(np.uint16)


def unstriped(offs):
    return offs[:16].T.reshape(-1).astype(np.int64)


E2M1 = np.array([0.0, 0.5, 1.0, 1.5, 2.0, 3.0, 4.0, 6.0, -0.0, -0.5, -1.0, -1.5, -2.0, -3.0, -4.0, -6.0])


def pack_weight(w, fmt):
    k, n = w.shape
    w = f64(np.asarray(w, np.float32).astype(ml_dtypes.bfloat16)).reshape(k // 32, 32, n)
    amax = np.abs(w).max(1)
    if fmt == "e4m3":
        byte = np.frexp(amax)[1] - 1 + 127 - 7
    else:
        mant, ex = np.frexp(amax / 6.0)
        byte = np.where(mant > 0.5, ex, ex - 1) + 127
    byte = np.clip(np.where(amax > 0, byte, 1), 1, 254)
    scaled = (w * np.exp2(127.0 - byte)[:, None, :]).reshape(k, n).astype(np.float32)
    by_word = np.ascontiguousarray(scaled.reshape(k // 512, 128, 4, n).transpose(0, 1, 3, 2))
    if fmt == "e4m3":
        words = by_word.astype(ml_dtypes.float8_e4m3fn).view(np.uint8)
    else:
        c = by_word.astype(ml_dtypes.float4_e2m1fn).view(np.uint8) & 0xF
        words = (c[..., 0::2] | (c[..., 1::2] << 4)).reshape(k // 512, 128, 2 * n)
    return np.ascontiguousarray(words), np.ascontiguousarray(byte.astype(np.uint8).reshape(k // 512, 16, n))


def unpack_weight(words, scales, fmt):
    g, _, n = scales.shape
    words = np.ascontiguousarray(words).reshape(g, 128, n, -1)
    if fmt == "e4m3":
        vals = words.view(ml_dtypes.float8_e4m3fn).astype(np.float64)
    else:
        nib = np.empty((g, 128, n, 4), np.uint8)
        nib[..., 0::2] = words & 0xF
        nib[..., 1::2] = words >> 4
        vals = E2M1[nib]
    vals = vals * np.repeat(np.exp2(scales.astype(np.float64) - 127.0), 8, axis=1)[..., None]
    return vals.transpose(0, 1, 3, 2).reshape(g * 512, n)


def gelu(v):
    return 0.5 * v * (1.0 + np.tanh(np.sqrt(2.0 / np.pi) * (v + 0.044715 * v**3)))


def bf(x):
    return np.asarray(x, np.float32).astype(ml_dtypes.bfloat16)


def planes(Y):
    n, m = Y.shape
    b = f64(bf(Y)).reshape(n // 32, 32, m)
    amax = np.abs(b).max(1)
    byte = np.clip(np.where(amax > 0, np.frexp(amax)[1] - 1 + 127 - 7, 1), 1, 254)
    codes = (b * np.exp2(127.0 - byte)[:, None, :]).reshape(n, m).astype(np.float32).astype(ml_dtypes.float8_e4m3fn).view(np.uint8)
    words = codes.reshape(n // 512, 128, 4, m).transpose(0, 1, 3, 2)
    return np.ascontiguousarray(words), np.ascontiguousarray(byte.astype(np.uint8).reshape(n // 512, 16, m))


K, K2, T, TB, S, H, T2, P, N = 1024, 512, 2048, 1024, 512, 1024, 2048, 1024, 512


def setup_inputs():
    n = np.random.standard_normal
    s, s2, u = mx_kscale(K)[:, None], mx_kscale(K2)[:, None], mx_kscale(H)[:, None]
    perm = np.random.permutation(T2)
    d = {}
    d["tab_words"], d["tab_scales"] = pack_weight(n((K, T)) * s, "e4m3")
    d["tab2_words"], d["tab2_scales"] = pack_weight(n((K2, TB)) * s2, "e4m3")
    d["offs"] = striped(np.random.permutation(T)[:S])
    d["offs2"] = striped(np.random.permutation(TB)[:S])
    d["offs3"] = striped(perm[:S])
    d["offs4"] = striped(perm[S:2 * S])
    d["offs5"] = striped(np.random.permutation(T2)[:P])
    d["w1"] = (0.56 * n((K, H)) / s / K**0.5).astype(np.float32)
    d["w2_words"], d["w2_scales"] = pack_weight(0.5 * n((K2, H)) / s2 / K2**0.5, "e2m1")
    d["wg1"] = np.exp(0.3 * n((128, S))).astype(np.float32)
    d["wg2"] = np.exp(0.3 * n((128, S))).astype(np.float32)
    d["page0"] = (0.5 * n((H, T2))).astype(np.float32)
    d["gain"] = (2.0 * np.exp(0.3 * n(H)) * u[:, 0]).astype(np.float32)
    d["w3"] = (n((H, N)) / u / H**0.5 * np.exp(0.8 * n(N))).astype(np.float32)
    d["w4_words"], d["w4_scales"] = pack_weight(1.5 * n((H, N)) / u / H**0.5, "e4m3")
    return d


def reference(tab_words, tab_scales, tab2_words, tab2_scales, offs, offs2, offs3, offs4, offs5,
              w1, w2_words, w2_scales, wg1, wg2, page0, gain, w3, w4_words, w4_scales):
    v = unpack_weight(tab_words, tab_scales, "e4m3")[:, unstriped(offs)]
    v2 = unpack_weight(tab2_words, tab2_scales, "e4m3")[:, unstriped(offs2)]
    h1 = np.sin(mxq(f64(w1), 0, "e4m3").T @ v)
    h2 = np.abs(unpack_weight(w2_words, w2_scales, "e2m1").T @ v2)
    page = f64(page0).copy()
    page[:, unstriped(offs3)] = np.tile(f64(wg1), (H // 128, 1)) * h1
    page[:, unstriped(offs4)] = np.tile(f64(wg2), (H // 128, 1)) * h2
    x = f64(gain)[:, None] * page[:, unstriped(offs5)]
    xq = mxq(x, 0, "e4m3")
    ya = mxq(f64(w3), 0, "e4m3").T @ xq
    yb = unpack_weight(w4_words, w4_scales, "e4m3").T @ xq
    y = ya / np.sqrt(1.0 + np.square(yb))
    words, scales = planes(y)
    return y, words, scales

@@ -1,0 +1,391 @@
+import math
+from contextlib import ExitStack
+
+import concourse.mybir as mybir
+
+K, K2, T, TB, S, H, T2, PICKS, N = 1024, 512, 2048, 1024, 512, 1024, 2048, 1024, 512
+FLOPS = 2 * (K * H * S + K2 * H * S + 2 * H * N * PICKS)
+
+F32 = mybir.dt.float32
+BF16 = mybir.dt.bfloat16
+I32 = mybir.dt.int32
+U32 = mybir.dt.uint32
+U16 = mybir.dt.uint16
+U8 = mybir.dt.uint8
+FP8X4 = mybir.dt.float8_e4m3fn_x4
+FP4X4 = mybir.dt.float4_e2m1fn_x4
+ACT = mybir.ActivationFunctionType
+MULT = mybir.AluOpType.mult
+ADD = mybir.AluOpType.add
+
+P = 128
+PACK = 4
+PASS = P * PACK
+ROW_TILES = H // P
+CHUNK = 256
+CHUNKS = PICKS // CHUNK
+QUADS = 4
+
+
+def tile_list_gas_well_board_kernel(
+    tc, tab_words, tab_scales, tab2_words, tab2_scales, offs, offs2, offs3, offs4, offs5,
+    w1, w2_words, w2_scales, wg1, wg2, page0, gain, w3, w4_words, w4_scales, out_0, out_1, out_2,
+):
+    nc = tc.nc
+    with ExitStack() as ctx:
+        keep = ctx.enter_context(tc.tile_pool(name="keep", bufs=1))
+        psum = ctx.enter_context(tc.psum_pool(name="psum", bufs=1))
+
+        def kept(name, shape, dtype):
+            return keep.tile(shape, dtype, name=name, align_bytes=64)
+
+        banks = [psum.tile([P, PASS], F32, name="bank%d" % n) for n in range(8)]
+
+        def load_list(name, src):
+            tile = keep.tile(list(src.shape), U16, name=name)
+            nc.sync.dma_start(tile[:], src)
+            return tile
+
+        def load_words(name, src):
+            tile = kept(name, [P, src.shape[1]], U32)
+            nc.sync.dma_start(tile[:].bitcast(I32), src.rearrange("p c i -> p (c i)").bitcast(I32))
+            return tile
+
+        def cleared_scales(name, src):
+            tile = kept(name, [P, src.shape[2]], U8)
+            nc.vector.memset(tile[:].bitcast(I32), 0)
+            return tile
+
+        def load_scales(tile, src):
+            passes = src.shape[0]
+            for q in range(QUADS):
+                nc.sync.dma_start(
+                    tile[32 * q : 32 * q + 4 * passes, :].bitcast(I32),
+                    src[:, 4 * q : 4 * q + 4, :].bitcast(I32),
+                )
+
+        def load_gate(tile, src, t0, t1):
+            rows = src.rearrange("(q t) s -> q t s", t=PACK)
+            view = tile[:, 0 : (t1 - t0) * S].rearrange("p (t s) -> p t s", s=S)
+            for q in range(QUADS):
+                nc.sync.dma_start(view[32 * q : 32 * q + 32, :, :], rows[:, t0:t1, :])
+            return view
+
+        wide = [kept("wide%d" % n, [P, PACK * PASS], F32) for n in range(3)]
+        rounded = [kept("rounded%d" % n, [P, PACK * PASS], BF16) for n in range(3)]
+        rows_h = [kept("rows_h%d" % n, [P, 2, S], F32) for n in range(4)]
+        picked = [kept("picked%d" % n, [P, PICKS], F32) for n in range(3)]
+        spare = kept("spare", [P, 2 * S], F32)
+        turns = [spare[:], picked[2][:], spare[:], wide[0][:, 0 : 2 * S]]
+        shared = kept("shared", [P, PACK * S], F32)
+
+        pages = {}
+
+        def load_page(i):
+            b, t = divmod(i, PACK)
+            pages[i] = kept("page%d" % i, [P, T2], F32)
+            nc.sync.dma_start(pages[i][:], page0.rearrange("(b p t) c -> b t p c", p=P, t=PACK)[b, t])
+
+        def load_weight(raw, rows):
+            nc.sync.dma_start(raw[:].rearrange("p (j c) -> p j c", j=PACK), rows.rearrange("(p j) c -> p j c", j=PACK))
+            return raw
+
+        def round_weight(dealt, raw):
+            nc.scalar.copy(
+                dealt[:].rearrange("p (t m j) -> p m t j", t=PACK, j=PACK),
+                raw[:].rearrange("p (j m t) -> p m t j", j=PACK, t=PACK),
+            )
+            return dealt[:]
+
+        def quantize(name, rounded):
+            width = rounded.shape[1] // PACK
+            codes = kept(name + "_codes", [P, width], U32)
+            scales = kept(name + "_scales", [P, width], U8)
+            nc.vector.quantize_mx(out=codes[:].bitcast(FP8X4), scales=scales[:], in_=rounded)
+            return codes, scales
+
+        def gather(name, table, offsets, dtype):
+            picked = kept(name, [P, S], dtype)
+            nc.vector.tensor_copy(picked[:], table[:].indirect(offsets[:]))
+            return picked
+
+        tab2_s = cleared_scales("tab2_s", tab2_scales)
+        w2_s = cleared_scales("w2_s", w2_scales)
+        tab_s = cleared_scales("tab_s", tab_scales)
+        w4_s = cleared_scales("w4_s", w4_scales)
+        one = kept("one", [P, 1], F32)
+        nc.vector.memset(one[:], 1.0)
+        quarter_turn = kept("quarter_turn", [P, 1], F32)
+        nc.vector.tensor_scalar(quarter_turn[:], one[:], math.pi / 2, None, MULT)
+        minus_quarter_turn = kept("minus_quarter_turn", [P, 1], F32)
+        nc.vector.tensor_scalar(minus_quarter_turn[:], one[:], -math.pi / 2, None, MULT)
+        warm = kept("warm", [P, 1], F32)
+        nc.scalar.activation(warm[:], one[:], ACT.Sin)
+        list2 = load_list("list2", offs2)
+        tab2_w = load_words("tab2_w", tab2_words[0])
+        w2_w = kept("w2_w", [P, 2 * H], U8)
+        nc.sync.dma_start(w2_w[:].bitcast(I32), w2_words[0].bitcast(I32))
+        list4 = load_list("list4", offs4)
+        load_scales(tab2_s, tab2_scales)
+        load_page(0)
+        load_scales(w2_s, w2_scales)
+        gate2_first = load_gate(kept("gate2_first", [P, S], F32), wg2, 0, 1)
+        load_page(1)
+        gate2_rest = load_gate(shared, wg2, 1, PACK)
+        load_page(2)
+        load_page(3)
+        list1 = load_list("list1", offs)
+        list3 = load_list("list3", offs3)
+        list5 = load_list("list5", offs5)
+        gains = kept("gains", [P, 2, PACK], F32)
+        nc.sync.dma_start(gains[:], gain.rearrange("(b p t) -> p b t", p=P, t=PACK))
+        tab_w = [load_words("tab_w0", tab_words[0])]
+        load_page(4)
+        tab_w.append(load_words("tab_w1", tab_words[1]))
+        load_scales(tab_s, tab_scales)
+        load_page(5)
+        w1_raw = {}
+        for a in range(2):
+            w1_raw[a, 0] = load_weight(wide[a], w1[a * PASS : (a + 1) * PASS, 0:PASS])
+        load_page(6)
+        load_page(7)
+        gate1 = [load_gate(kept("gate1_0", [P, 2 * S], F32), wg1, 0, 2)]
+        w1_raw[0, 1] = load_weight(wide[2], w1[0:PASS, PASS:H])
+
+        v2_w = gather("v2_w", tab2_w, list2, U32)
+        w2_dealt = [kept("w2_dealt%d" % b, [P, 2 * PASS], U8) for b in range(2)]
+        w2_s_dealt = [kept("w2_s_dealt%d" % b, [P, PASS], U8) for b in range(2)]
+
+        def deal_w2_words(b):
+            nc.vector.tensor_copy(
+                w2_dealt[b][:].rearrange("p (t o i e) -> p o t i e", t=PACK, i=8, e=2),
+                w2_w[:, 2 * PASS * b : 2 * PASS * (b + 1)].rearrange("p (o i t e) -> p o t i e", t=PACK, i=8, e=2),
+            )
+
+        def deal_scales(dst, src):
+            nc.vector.tensor_copy(
+                dst.rearrange("p (t o i) -> p o t i", t=PACK, i=16),
+                src.rearrange("p (o i t) -> p o t i", t=PACK, i=16),
+            )
+
+        deal_w2_words(0)
+        v2_s = gather("v2_s", tab2_s, list2, U8)
+        deal_scales(w2_s_dealt[0][:], w2_s[:, 0:PASS])
+        deal_w2_words(1)
+        deal_scales(w2_s_dealt[1][:], w2_s[:, PASS:H])
+
+        def scatter(i, offsets, h, gate):
+            nc.vector.tensor_tensor(pages[i][:].indirect(offsets[:]), h, gate, MULT)
+
+        def put_h2(i, h):
+            b, t = divmod(i, PACK)
+            acc = banks[i]
+            nc.tensor.matmul_mx(
+                out=acc[:],
+                lhsT=w2_dealt[b][:, 2 * P * t : 2 * P * (t + 1)].bitcast(FP4X4),
+                lhsT_scale=w2_s_dealt[b][:, P * t : P * (t + 1)],
+                rhs=v2_w[:].bitcast(FP8X4), rhs_scale=v2_s[:], start=True, stop=True,
+            )
+            nc.scalar.activation(h, acc[:], ACT.Abs)
+            scatter(i, list4, h, gate2_first[:, 0, :] if t == 0 else gate2_rest[:, t - 1, :])
+
+        for i in range(4):
+            put_h2(i, rows_h[i // 2][:, i % 2, :])
+        v1_w = [gather("v1_w0", tab_w[0], list1, U32)]
+        put_h2(4, rows_h[2][:, 0, :])
+        v1_w.append(gather("v1_w1", tab_w[1], list1, U32))
+        v1_s = gather("v1_s", tab_s, list1, U8)
+        put_h2(5, rows_h[2][:, 1, :])
+
+        w1_q = {}
+
+        def make_w1(b):
+            for a in range(2):
+                w1_q[a, b] = quantize("w1_%d%d" % (a, b), round_weight(rounded[(2 * b + a) % 3], w1_raw[a, b]))
+
+        def reduce_h1(pair):
+            dist = rows_h[pair]
+            flat = dist[:].rearrange("p u s -> p (u s)")
+            for u in range(2):
+                i = 2 * pair + u
+                b, t = divmod(i, PACK)
+                acc = banks[i]
+                for a in range(2):
+                    codes, scales = w1_q[a, b]
+                    nc.tensor.matmul_mx(
+                        out=acc[:],
+                        lhsT=codes[:, P * t : P * (t + 1)].bitcast(FP8X4), lhsT_scale=scales[:, P * t : P * (t + 1)],
+                        rhs=v1_w[a][:].bitcast(FP8X4), rhs_scale=v1_s[4 * a : P, :],
+                        start=(a == 0), stop=(a == 1),
+                    )
+                nc.scalar.activation(dist[:, u, :], acc[:], ACT.Abs, bias=minus_quarter_turn[:])
+            nc.scalar.activation(turns[pair].bitcast(U32), flat, ACT.Copy, scale=1 / (2 * math.pi), bias=-0.25)
+            nc.vector.scalar_tensor_tensor(flat, turns[pair].bitcast(I32), -2 * math.pi, flat, MULT, ADD)
+
+        def sine(out, src):
+            nc.scalar.activation(out, src, ACT.Sin, scale=-1.0, bias=quarter_turn[:])
+
+        def put_h1(i, h):
+            scatter(i, list3, h, gate1[i % PACK // 2][:, i % 2, :])
+
+        planes = shared[:].bitcast(BF16).rearrange("p (c t j) -> p c t j", c=CHUNKS, t=PACK)
+
+        def fetch(i):
+            b, t = divmod(i, PACK)
+            nc.vector.tensor_copy(picked[i % 3][:], pages[i][:].indirect(list5[:]))
+            nc.scalar.activation(
+                planes[:, :, t, :], picked[i % 3][:].rearrange("p (c j) -> p c j", c=CHUNKS),
+                ACT.Copy, scale=gains[:, b, t : t + 1],
+            )
+
+        def weave(engine_copy, dst, src):
+            engine_copy(dst.rearrange("p (c i t) -> p c t i", i=4, t=PACK), src.rearrange("p t (c i) -> p c t i", i=4))
+
+        make_w1(0)
+        put_h2(6, wide[1][:, 0:S])
+        reduce_h1(0)
+        put_h2(7, rows_h[3][:, 1, :])
+        reduce_h1(1)
+        w1_raw[1, 1] = load_weight(wide[0], w1[PASS:K, PASS:H])
+        w4_w = [load_words("w4_w%d" % a, w4_words[a]) for a in range(2)]
+        load_scales(w4_s, w4_scales)
+        w3_raw = [load_weight(wide[1], w3[0:PASS, :])]
+        gate1.append(load_gate(kept("gate1_1", [P, 2 * S], F32), wg1, 2, 4))
+        sine(rows_h[0][:], rows_h[0][:])
+        put_h1(0, rows_h[0][:, 0, :])
+        put_h1(1, rows_h[0][:, 1, :])
+        make_w1(1)
+        w3_raw.append(load_weight(wide[2], w3[PASS:H, :]))
+        sine(rows_h[1][:], rows_h[1][:])
+        reduce_h1(2)
+        reduce_h1(3)
+        w3_q = [quantize("w3_%d" % a, round_weight(rounded[1 + a], w3_raw[a])) for a in range(2)]
+        fetch(0)
+        fetch(1)
+        put_h1(2, rows_h[1][:, 0, :])
+        put_h1(3, rows_h[1][:, 1, :])
+        sine(rows_h[2][:], rows_h[2][:])
+        sine(rows_h[3][:, 0, :], rows_h[3][:, 0, :])
+        fetch(2)
+        fetch(3)
+        put_h1(4, rows_h[2][:, 0, :])
+        put_h1(5, rows_h[2][:, 1, :])
+
+        w4_dealt = [kept("w4_dealt%d" % a, [P, N], U32) for a in range(2)]
+        for a in range(2):
+            nc.vector.tensor_copy(
+                w4_dealt[a][:].bitcast(I32).rearrange("p (t o i) -> p o t i", t=PACK, i=4),
+                w4_w[a][:].bitcast(I32).rearrange("p (o i t) -> p o t i", t=PACK, i=4),
+            )
+        w4_s_dealt = kept("w4_s_dealt", [P, N], U8)
+        deal_scales(w4_s_dealt[:], w4_s[:])
+        for c in (2, 3, 0, 1):
+            weave(nc.scalar.copy, rounded[c // 2][:, PICKS * (c % 2) : PICKS * (c % 2 + 1)], planes[:, c])
+        put_h1(6, rows_h[3][:, 0, :])
+        fetch(4)
+        sine(picked[1][:, 0:S], rows_h[3][:, 1, :])
+        nc.scalar.activation(warm[:], picked[1][:, 0:1], ACT.Abs_reciprocal_sqrt, bias=one[:])
+        fetch(5)
+        x0_q = {1: quantize("x0_1", rounded[1][:])}
+        x0_q[0] = quantize("x0_0", rounded[0][:])
+        fetch(6)
+        put_h1(7, picked[1][:, 0:S])
+        x1_woven = []
+        for c in range(CHUNKS):
+            woven = kept("x1_woven%d" % c, [P, CHUNK * PACK], BF16)
+            weave(nc.scalar.copy, woven[:], planes[:, c])
+            x1_woven.append(woven)
+
+        accs = {}
+
+        def second_stage(c, a, x_codes, x_scales):
+            for side in (1, 0):
+                for h in range(2):
+                    accs[c, side, h] = banks[4 * (c % 2) + 2 * side + h][:].rearrange("p (u j) -> p u j", u=2)
+                    for u in range(2):
+                        cols = slice(P * (2 * h + u), P * (2 * h + u + 1))
+                        if side == 0:
+                            codes, scales = w3_q[a][0][:, cols], w3_q[a][1][:, cols]
+                        else:
+                            codes, scales = w4_dealt[a][:, cols], w4_s_dealt[4 * a : P, cols]
+                        nc.tensor.matmul_mx(
+                            out=accs[c, side, h][:, u, :], lhsT=codes.bitcast(FP8X4), lhsT_scale=scales,
+                            rhs=x_codes.bitcast(FP8X4), rhs_scale=x_scales,
+                            start=(a == 0 and u == 0), stop=(a == 1 and u == 1),
+                        )
+
+        def first_pass(c):
+            codes, scales = x0_q[c // 2]
+            cols = slice(CHUNK * (c % 2), CHUNK * (c % 2 + 1))
+            second_stage(c, 0, codes[:, cols], scales[:, cols])
+
+        last = [rows_h[0][:, 0, 0:CHUNK]] + [shared[:, S * c : S * c + CHUNK] for c in range(CHUNKS - 1)]
+
+        def fetch_last(c):
+            i = ROW_TILES - 1
+            nc.vector.tensor_copy(last[c], pages[i][:].indirect(list5[:, 16 * c : 16 * (c + 1)]))
+
+        def scale_last(c):
+            nc.vector.tensor_scalar(
+                x1_woven[c][:].rearrange("p (c t) -> p c t", t=PACK)[:, :, 3],
+                last[c], gains[:, 1, 3:4], None, MULT,
+            )
+
+        def second_pass(c):
+            codes, scales = quantize("x1_%d" % c, x1_woven[c][:])
+            second_stage(c, 1, codes[:], scales[:])
+
+        y_scales = kept("y_scales", [P, PICKS], U8)
+        y_rows = out_0.rearrange("(p t) j -> p t j", t=PACK)
+        y_words = out_1[0].rearrange("p m t -> p (m t)").bitcast(I32)
+        results = {}
+
+        def combine(c):
+            damp = picked[c % 3][:].rearrange("p (t c) -> p t c", t=PACK)
+            y = rows_h[1 + c % 3][:].rearrange("p u (v c) -> p (u v) c", v=2)
+            for h in range(2):
+                part = slice(2 * h, 2 * h + 2)
+                nc.scalar.activation(damp[:, part, :], accs[c, 1, h][:], ACT.Square)
+                nc.scalar.activation(damp[:, part, :], damp[:, part, :], ACT.Abs_reciprocal_sqrt, bias=one[:])
+                nc.vector.tensor_tensor(y[:, part, :], accs[c, 0, h][:], damp[:, part, :], MULT)
+            nc.sync.dma_start(y_rows[:, :, CHUNK * c : CHUNK * (c + 1)], y)
+            results[c] = y
+
+        def hand_out(c):
+            cols = slice(CHUNK * c, CHUNK * (c + 1))
+            woven = x1_woven[c][:]
+            weave(nc.scalar.copy if c == 2 else nc.vector.tensor_copy, woven, results[c])
+            codes = kept("y_codes%d" % c, [P, CHUNK], U32)
+            nc.vector.quantize_mx(
+                out=codes[:].bitcast(FP8X4), scales=y_scales[:, cols], in_=woven
+            )
+            nc.sync.dma_start(y_words[:, cols], codes[:].bitcast(I32))
+
+        first_pass(0)
+        first_pass(1)
+        fetch_last(0)
+        scale_last(0)
+        fetch_last(1)
+        second_pass(0)
+        scale_last(1)
+        fetch_last(2)
+        second_pass(1)
+        scale_last(2)
+        fetch_last(3)
+        scale_last(3)
+        combine(0)
+        first_pass(2)
+        second_pass(2)
+        combine(1)
+        hand_out(0)
+        first_pass(3)
+        second_pass(3)
+        hand_out(1)
+        combine(2)
+        combine(3)
+        hand_out(2)
+        hand_out(3)
+        for q in range(QUADS):
+            nc.sync.dma_start(
+                out_2[0, 4 * q : 4 * q + 4, :].bitcast(I32), y_scales[32 * q : 32 * q + 4, :].bitcast(I32)
+            )

@@ -2,6 +2,7 @@ import math
 from contextlib import ExitStack
 
 import concourse.mybir as mybir
+from concourse.masks import make_identity
 
 K, K2, T, TB, S, H, T2, PICKS, N = 1024, 512, 2048, 1024, 512, 1024, 2048, 1024, 512
 FLOPS = 2 * (K * H * S + K2 * H * S + 2 * H * N * PICKS)
@@ -64,20 +65,35 @@ def tile_list_gas_well_board_kernel(
                     src[:, 4 * q : 4 * q + 4, :].bitcast(I32),
                 )
 
-        def load_gate(tile, src, t0, t1):
-            rows = src.rearrange("(q t) s -> q t s", t=PACK)
-            view = tile[:, 0 : (t1 - t0) * S].rearrange("p (t s) -> p t s", s=S)
-            for q in range(QUADS):
-                nc.sync.dma_start(view[32 * q : 32 * q + 32, :, :], rows[:, t0:t1, :])
-            return view
-
         wide = [kept("wide%d" % n, [P, PACK * PASS], F32) for n in range(3)]
         rounded = [kept("rounded%d" % n, [P, PACK * PASS], BF16) for n in range(3)]
         rows_h = [kept("rows_h%d" % n, [P, 2, S], F32) for n in range(4)]
-        picked = [kept("picked%d" % n, [P, PICKS], F32) for n in range(3)]
-        spare = kept("spare", [P, 2 * S], F32)
-        turns = [spare[:], picked[2][:], spare[:], wide[0][:, 0 : 2 * S]]
+        fetched = kept("fetched", [P, 3 * PICKS], F32)
+        picked = [fetched[:, PICKS * n : PICKS * (n + 1)] for n in range(3)]
         shared = kept("shared", [P, PACK * S], F32)
+        gate1 = kept("gate1", [P, PACK * S], F32)
+        dist = kept("dist", [P, PACK * S], F32)
+        x1_woven = kept("x1_woven", [P, PACK * PICKS], BF16)
+        turns = x1_woven[:].bitcast(F32)
+        identity = kept("identity", [P, P], F32)
+        make_identity(nc, identity[:])
+        gate_rows = rounded[2][:].bitcast(F32)
+
+        def turn_gate(rows):
+            for n in range(S // P):
+                nc.tensor.transpose(banks[7][:, P * n : P * (n + 1)], rows[:, P * n : P * (n + 1)], identity[:])
+
+        def deal_gate(gate, t):
+            spread = picked[2][:, 0:S]
+            nc.scalar.copy(
+                spread.rearrange("p (n a q) -> p n a q", a=QUADS, q=32),
+                banks[7][:].rearrange("p (n q t) -> p n t q", q=32, t=PACK)[:, :, t, :]
+                .unsqueeze(2).to_broadcast([P, S // P, QUADS, 32]),
+            )
+            acc = banks[4 + t % 3]
+            for n in range(S // P):
+                nc.tensor.transpose(acc[:, P * n : P * (n + 1)], spread[:, P * n : P * (n + 1)], identity[:])
+            nc.scalar.copy(gate[:, S * t : S * (t + 1)], acc[:])
 
         pages = {}
 
@@ -87,22 +103,28 @@ def tile_list_gas_well_board_kernel(
             nc.sync.dma_start(pages[i][:], page0.rearrange("(b p t) c -> b t p c", p=P, t=PACK)[b, t])
 
         def load_weight(raw, rows):
-            nc.sync.dma_start(raw[:].rearrange("p (j c) -> p j c", j=PACK), rows.rearrange("(p j) c -> p j c", j=PACK))
+            nc.sync.dma_start(raw.rearrange("p (j c) -> p j c", j=PACK), rows.rearrange("(p j) c -> p j c", j=PACK))
             return raw
 
         def round_weight(dealt, raw):
             nc.scalar.copy(
                 dealt[:].rearrange("p (t m j) -> p m t j", t=PACK, j=PACK),
-                raw[:].rearrange("p (j m t) -> p m t j", j=PACK, t=PACK),
+                raw.rearrange("p (j m t) -> p m t j", j=PACK, t=PACK),
             )
             return dealt[:]
 
-        def quantize(name, rounded):
-            width = rounded.shape[1] // PACK
-            codes = kept(name + "_codes", [P, width], U32)
-            scales = kept(name + "_scales", [P, width], U8)
-            nc.vector.quantize_mx(out=codes[:].bitcast(FP8X4), scales=scales[:], in_=rounded)
-            return codes, scales
+        def mx_tiles(name, width):
+            return kept(name + "_codes", [P, width], U32), kept(name + "_scales", [P, width], U8)
+
+        def quantize(tiles, src):
+            codes, scales = tiles
+            nc.vector.quantize_mx(out=codes[:].bitcast(FP8X4), scales=scales[:], in_=src)
+            return tiles
+
+        def weave(engine_copy, dst, src):
+            engine_copy(dst.rearrange("p (c i t) -> p c t i", i=4, t=PACK), src.rearrange("p t (c i) -> p c t i", i=4))
+
+        operands = [mx_tiles("operand%d" % n, PASS) for n in range(4)]
 
         def gather(name, table, offsets, dtype):
             picked = kept(name, [P, S], dtype)
@@ -122,35 +144,41 @@ def tile_list_gas_well_board_kernel(
         warm = kept("warm", [P, 1], F32)
         nc.scalar.activation(warm[:], one[:], ACT.Sin)
         list2 = load_list("list2", offs2)
-        tab2_w = load_words("tab2_w", tab2_words[0])
-        w2_w = kept("w2_w", [P, 2 * H], U8)
-        nc.sync.dma_start(w2_w[:].bitcast(I32), w2_words[0].bitcast(I32))
         list4 = load_list("list4", offs4)
-        load_scales(tab2_s, tab2_scales)
-        load_page(0)
-        load_scales(w2_s, w2_scales)
-        gate2_first = load_gate(kept("gate2_first", [P, S], F32), wg2, 0, 1)
-        load_page(1)
-        gate2_rest = load_gate(shared, wg2, 1, PACK)
-        load_page(2)
-        load_page(3)
         list1 = load_list("list1", offs)
         list3 = load_list("list3", offs3)
+        tab2_w = load_words("tab2_w", tab2_words[0])
+        w2_w = [kept("w2_w%d" % b, [P, 2 * PASS], U8) for b in range(2)]
+
+        def load_w2(b):
+            nc.sync.dma_start(w2_w[b][:].bitcast(I32), w2_words[0][:, 2 * PASS * b : 2 * PASS * (b + 1)].bitcast(I32))
+
+        load_w2(0)
+        load_scales(tab2_s, tab2_scales)
+        nc.sync.dma_start(gate_rows[:, 0:S], wg2)
+        load_scales(w2_s, w2_scales)
+        load_w2(1)
+        load_page(0)
+        load_page(1)
+        load_page(2)
+        nc.sync.dma_start(gate_rows[:, S : 2 * S], wg1)
         list5 = load_list("list5", offs5)
         gains = kept("gains", [P, 2, PACK], F32)
         nc.sync.dma_start(gains[:], gain.rearrange("(b p t) -> p b t", p=P, t=PACK))
+        load_page(3)
         tab_w = [load_words("tab_w0", tab_words[0])]
         load_page(4)
         tab_w.append(load_words("tab_w1", tab_words[1]))
         load_scales(tab_s, tab_scales)
-        load_page(5)
         w1_raw = {}
         for a in range(2):
-            w1_raw[a, 0] = load_weight(wide[a], w1[a * PASS : (a + 1) * PASS, 0:PASS])
+            w1_raw[a, 0] = load_weight(wide[a][:], w1[a * PASS : (a + 1) * PASS, 0:PASS])
+        load_page(5)
         load_page(6)
         load_page(7)
-        gate1 = [load_gate(kept("gate1_0", [P, 2 * S], F32), wg1, 0, 2)]
-        w1_raw[0, 1] = load_weight(wide[2], w1[0:PASS, PASS:H])
+        w4_w = [load_words("w4_w%d" % a, w4_words[a]) for a in range(2)]
+        load_scales(w4_s, w4_scales)
+        w1_raw[0, 1] = load_weight(wide[2][:], w1[0:PASS, PASS:H])
 
         v2_w = gather("v2_w", tab2_w, list2, U32)
         w2_dealt = [kept("w2_dealt%d" % b, [P, 2 * PASS], U8) for b in range(2)]
@@ -159,7 +187,7 @@ def tile_list_gas_well_board_kernel(
         def deal_w2_words(b):
             nc.vector.tensor_copy(
                 w2_dealt[b][:].rearrange("p (t o i e) -> p o t i e", t=PACK, i=8, e=2),
-                w2_w[:, 2 * PASS * b : 2 * PASS * (b + 1)].rearrange("p (o i t e) -> p o t i e", t=PACK, i=8, e=2),
+                w2_w[b][:].rearrange("p (o i t e) -> p o t i e", t=PACK, i=8, e=2),
             )
 
         def deal_scales(dst, src):
@@ -179,7 +207,7 @@ def tile_list_gas_well_board_kernel(
 
         def put_h2(i, h):
             b, t = divmod(i, PACK)
-            acc = banks[i]
+            acc = banks[t]
             nc.tensor.matmul_mx(
                 out=acc[:],
                 lhsT=w2_dealt[b][:, 2 * P * t : 2 * P * (t + 1)].bitcast(FP4X4),
@@ -187,90 +215,84 @@ def tile_list_gas_well_board_kernel(
                 rhs=v2_w[:].bitcast(FP8X4), rhs_scale=v2_s[:], start=True, stop=True,
             )
             nc.scalar.activation(h, acc[:], ACT.Abs)
-            scatter(i, list4, h, gate2_first[:, 0, :] if t == 0 else gate2_rest[:, t - 1, :])
+            scatter(i, list4, h, shared[:, S * t : S * (t + 1)])
 
+        turn_gate(gate_rows[:, 0:S])
         for i in range(4):
+            deal_gate(shared, i)
             put_h2(i, rows_h[i // 2][:, i % 2, :])
+        turn_gate(gate_rows[:, S : 2 * S])
+        for t in range(PACK):
+            deal_gate(gate1, t)
         v1_w = [gather("v1_w0", tab_w[0], list1, U32)]
         put_h2(4, rows_h[2][:, 0, :])
         v1_w.append(gather("v1_w1", tab_w[1], list1, U32))
         v1_s = gather("v1_s", tab_s, list1, U8)
-        put_h2(5, rows_h[2][:, 1, :])
 
         w1_q = {}
 
-        def make_w1(b):
+        def make_w1(a, b):
+            woven = rounded[(2 * b + a) % 3][:]
+            weave(nc.scalar.copy, woven, w1_raw[a, b].rearrange("p (j c) -> p j c", j=PACK))
+            w1_q[a, b] = quantize(operands[2 * b + a], woven)
+
+        def product_h1(b):
             for a in range(2):
-                w1_q[a, b] = quantize("w1_%d%d" % (a, b), round_weight(rounded[(2 * b + a) % 3], w1_raw[a, b]))
-
-        def reduce_h1(pair):
-            dist = rows_h[pair]
-            flat = dist[:].rearrange("p u s -> p (u s)")
-            for u in range(2):
-                i = 2 * pair + u
-                b, t = divmod(i, PACK)
-                acc = banks[i]
-                for a in range(2):
-                    codes, scales = w1_q[a, b]
+                codes, scales = w1_q[a, b]
+                for n in range(S // P):
+                    cols = slice(P * n, P * (n + 1))
                     nc.tensor.matmul_mx(
-                        out=acc[:],
-                        lhsT=codes[:, P * t : P * (t + 1)].bitcast(FP8X4), lhsT_scale=scales[:, P * t : P * (t + 1)],
-                        rhs=v1_w[a][:].bitcast(FP8X4), rhs_scale=v1_s[4 * a : P, :],
-                        start=(a == 0), stop=(a == 1),
+                        out=banks[n][:], lhsT=v1_w[a][:, cols].bitcast(FP8X4), lhsT_scale=v1_s[4 * a : P, cols],
+                        rhs=codes[:].bitcast(FP8X4), rhs_scale=scales[:], start=(a == 0), stop=(a == 1),
                     )
-                nc.scalar.activation(dist[:, u, :], acc[:], ACT.Abs, bias=minus_quarter_turn[:])
-            nc.scalar.activation(turns[pair].bitcast(U32), flat, ACT.Copy, scale=1 / (2 * math.pi), bias=-0.25)
-            nc.vector.scalar_tensor_tensor(flat, turns[pair].bitcast(I32), -2 * math.pi, flat, MULT, ADD)
+            for n in range(S // P):
+                nc.scalar.activation(
+                    dist[:, S * n : S * (n + 1)].rearrange("p (t m) -> p t m", t=PACK),
+                    banks[n][:].rearrange("p (m t) -> p t m", t=PACK),
+                    ACT.Abs, bias=minus_quarter_turn[:],
+                )
 
-        def sine(out, src):
-            nc.scalar.activation(out, src, ACT.Sin, scale=-1.0, bias=quarter_turn[:])
+        def reduce_h1(t0, t1):
+            cols = slice(S * t0, S * t1)
+            by_tile = dist[:].rearrange("p (n t m) -> p t n m", t=PACK, m=P)
+            nc.scalar.activation(
+                turns[:, cols].bitcast(U32).rearrange("p (t n m) -> p t n m", n=S // P, m=P), by_tile[:, t0:t1],
+                ACT.Copy, scale=1 / (2 * math.pi), bias=-0.25,
+            )
+            nc.scalar.activation(turns[:, cols], turns[:, cols].bitcast(U32), ACT.Copy, scale=-2 * math.pi)
+            for t in range(t0, t1):
+                for n in range(S // P):
+                    for src, first in ((by_tile[:, t, n], True), (turns[:, S * t + P * n : S * t + P * (n + 1)], False)):
+                        nc.tensor.matmul(
+                            banks[4 + t][:, P * n : P * (n + 1)], lhsT=src,
+                            rhs=identity[:], start=first, stop=not first, is_transpose=True,
+                        )
+
+        def sine(out, t):
+            nc.scalar.activation(out, banks[4 + t][:], ACT.Sin, scale=-1.0, bias=quarter_turn[:])
 
         def put_h1(i, h):
-            scatter(i, list3, h, gate1[i % PACK // 2][:, i % 2, :])
+            scatter(i, list3, h, gate1[:, S * (i % PACK) : S * (i % PACK + 1)])
 
         planes = shared[:].bitcast(BF16).rearrange("p (c t j) -> p c t j", c=CHUNKS, t=PACK)
 
         def fetch(i):
             b, t = divmod(i, PACK)
-            nc.vector.tensor_copy(picked[i % 3][:], pages[i][:].indirect(list5[:]))
+            nc.vector.tensor_copy(picked[i % 3], pages[i][:].indirect(list5[:]))
             nc.scalar.activation(
-                planes[:, :, t, :], picked[i % 3][:].rearrange("p (c j) -> p c j", c=CHUNKS),
+                planes[:, :, t, :], picked[i % 3].rearrange("p (c j) -> p c j", c=CHUNKS),
                 ACT.Copy, scale=gains[:, b, t : t + 1],
             )
 
-        def weave(engine_copy, dst, src):
-            engine_copy(dst.rearrange("p (c i t) -> p c t i", i=4, t=PACK), src.rearrange("p t (c i) -> p c t i", i=4))
+        def h_slot(i):
+            return rows_h[i // 2][:, i % 2, :]
 
-        make_w1(0)
-        put_h2(6, wide[1][:, 0:S])
-        reduce_h1(0)
-        put_h2(7, rows_h[3][:, 1, :])
-        reduce_h1(1)
-        w1_raw[1, 1] = load_weight(wide[0], w1[PASS:K, PASS:H])
-        w4_w = [load_words("w4_w%d" % a, w4_words[a]) for a in range(2)]
-        load_scales(w4_s, w4_scales)
-        w3_raw = [load_weight(wide[1], w3[0:PASS, :])]
-        gate1.append(load_gate(kept("gate1_1", [P, 2 * S], F32), wg1, 2, 4))
-        sine(rows_h[0][:], rows_h[0][:])
-        put_h1(0, rows_h[0][:, 0, :])
-        put_h1(1, rows_h[0][:, 1, :])
-        make_w1(1)
-        w3_raw.append(load_weight(wide[2], w3[PASS:H, :]))
-        sine(rows_h[1][:], rows_h[1][:])
-        reduce_h1(2)
-        reduce_h1(3)
-        w3_q = [quantize("w3_%d" % a, round_weight(rounded[1 + a], w3_raw[a])) for a in range(2)]
-        fetch(0)
-        fetch(1)
-        put_h1(2, rows_h[1][:, 0, :])
-        put_h1(3, rows_h[1][:, 1, :])
-        sine(rows_h[2][:], rows_h[2][:])
-        sine(rows_h[3][:, 0, :], rows_h[3][:, 0, :])
-        fetch(2)
-        fetch(3)
-        put_h1(4, rows_h[2][:, 0, :])
-        put_h1(5, rows_h[2][:, 1, :])
-
+        make_w1(0, 0)
+        make_w1(1, 0)
+        put_h2(5, wide[1][:, 0:S])
+        put_h2(6, h_slot(6))
+        put_h2(7, h_slot(7))
+        product_h1(0)
         w4_dealt = [kept("w4_dealt%d" % a, [P, N], U32) for a in range(2)]
         for a in range(2):
             nc.vector.tensor_copy(
@@ -279,22 +301,48 @@ def tile_list_gas_well_board_kernel(
             )
         w4_s_dealt = kept("w4_s_dealt", [P, N], U8)
         deal_scales(w4_s_dealt[:], w4_s[:])
+        w1_raw[1, 1] = load_weight(fetched[:, 0 : 2 * PICKS], w1[PASS:K, PASS:H])
+        w3_raw = [load_weight(wide[0][:], w3[0:PASS, :])]
+        reduce_h1(0, 1)
+        reduce_h1(1, 2)
+        sine(h_slot(0), 0)
+        sine(h_slot(1), 1)
+        put_h1(0, h_slot(0))
+        put_h1(1, h_slot(1))
+        reduce_h1(2, 4)
+        make_w1(0, 1)
+        make_w1(1, 1)
+        sine(h_slot(2), 2)
+        sine(h_slot(3), 3)
+        product_h1(1)
+        reduce_h1(0, 2)
+        reduce_h1(2, 4)
+        w3_raw.append(load_weight(dist[:], w3[PASS:H, :]))
+        for t in range(3):
+            sine(h_slot(4 + t), t)
+        fetch(0)
+        fetch(1)
+        put_h1(2, h_slot(2))
+        put_h1(3, h_slot(3))
+        w3_q = [quantize(operands[a], round_weight(rounded[1 + a], w3_raw[a])) for a in range(2)]
+        fetch(2)
+        fetch(3)
+        put_h1(4, h_slot(4))
+        put_h1(5, h_slot(5))
         for c in (2, 3, 0, 1):
             weave(nc.scalar.copy, rounded[c // 2][:, PICKS * (c % 2) : PICKS * (c % 2 + 1)], planes[:, c])
-        put_h1(6, rows_h[3][:, 0, :])
+        put_h1(6, h_slot(6))
         fetch(4)
-        sine(picked[1][:, 0:S], rows_h[3][:, 1, :])
+        sine(picked[1][:, 0:S], 3)
         nc.scalar.activation(warm[:], picked[1][:, 0:1], ACT.Abs_reciprocal_sqrt, bias=one[:])
         fetch(5)
-        x0_q = {1: quantize("x0_1", rounded[1][:])}
-        x0_q[0] = quantize("x0_0", rounded[0][:])
+        x0_q = {1: quantize(operands[3], rounded[1][:])}
+        x0_q[0] = quantize(operands[2], rounded[0][:])
         fetch(6)
         put_h1(7, picked[1][:, 0:S])
-        x1_woven = []
+        woven_chunks = [x1_woven[:, PICKS * c : PICKS * (c + 1)] for c in range(CHUNKS)]
         for c in range(CHUNKS):
-            woven = kept("x1_woven%d" % c, [P, CHUNK * PACK], BF16)
-            weave(nc.scalar.copy, woven[:], planes[:, c])
-            x1_woven.append(woven)
+            weave(nc.scalar.copy, woven_chunks[c], planes[:, c])
 
         accs = {}
 
@@ -327,12 +375,12 @@ def tile_list_gas_well_board_kernel(
 
         def scale_last(c):
             nc.vector.tensor_scalar(
-                x1_woven[c][:].rearrange("p (c t) -> p c t", t=PACK)[:, :, 3],
+                woven_chunks[c].rearrange("p (c t) -> p c t", t=PACK)[:, :, 3],
                 last[c], gains[:, 1, 3:4], None, MULT,
             )
 
         def second_pass(c):
-            codes, scales = quantize("x1_%d" % c, x1_woven[c][:])
+            codes, scales = quantize(mx_tiles("x1_%d" % c, CHUNK), woven_chunks[c])
             second_stage(c, 1, codes[:], scales[:])
 
         y_scales = kept("y_scales", [P, PICKS], U8)
@@ -341,7 +389,7 @@ def tile_list_gas_well_board_kernel(
         results = {}
 
         def combine(c):
-            damp = picked[c % 3][:].rearrange("p (t c) -> p t c", t=PACK)
+            damp = picked[c % 3].rearrange("p (t c) -> p t c", t=PACK)
             y = rows_h[1 + c % 3][:].rearrange("p u (v c) -> p (u v) c", v=2)
             for h in range(2):
                 part = slice(2 * h, 2 * h + 2)
@@ -353,7 +401,7 @@ def tile_list_gas_well_board_kernel(
 
         def hand_out(c):
             cols = slice(CHUNK * c, CHUNK * (c + 1))
-            woven = x1_woven[c][:]
+            woven = woven_chunks[c]
             weave(nc.scalar.copy if c == 2 else nc.vector.tensor_copy, woven, results[c])
             codes = kept("y_codes%d" % c, [P, CHUNK], U32)
             nc.vector.quantize_mx(

@@ -144,9 +144,6 @@ def tile_list_gas_well_board_kernel(
         warm = kept("warm", [P, 1], F32)
         nc.scalar.activation(warm[:], one[:], ACT.Sin)
         list2 = load_list("list2", offs2)
-        list4 = load_list("list4", offs4)
-        list1 = load_list("list1", offs)
-        list3 = load_list("list3", offs3)
         tab2_w = load_words("tab2_w", tab2_words[0])
         w2_w = [kept("w2_w%d" % b, [P, 2 * PASS], U8) for b in range(2)]
 
@@ -154,14 +151,17 @@ def tile_list_gas_well_board_kernel(
             nc.sync.dma_start(w2_w[b][:].bitcast(I32), w2_words[0][:, 2 * PASS * b : 2 * PASS * (b + 1)].bitcast(I32))
 
         load_w2(0)
-        load_scales(tab2_s, tab2_scales)
         nc.sync.dma_start(gate_rows[:, 0:S], wg2)
+        list4 = load_list("list4", offs4)
+        load_scales(tab2_s, tab2_scales)
         load_scales(w2_s, w2_scales)
         load_w2(1)
         load_page(0)
         load_page(1)
         load_page(2)
         nc.sync.dma_start(gate_rows[:, S : 2 * S], wg1)
+        list1 = load_list("list1", offs)
+        list3 = load_list("list3", offs3)
         list5 = load_list("list5", offs5)
         gains = kept("gains", [P, 2, PACK], F32)
         nc.sync.dma_start(gains[:], gain.rearrange("(b p t) -> p b t", p=P, t=PACK))
@@ -232,7 +232,7 @@ def tile_list_gas_well_board_kernel(
         w1_q = {}
 
         def make_w1(a, b):
-            woven = rounded[(2 * b + a) % 3][:]
+            woven = (rounded[0][:], rounded[1][:], x1_woven[:, 0 : PACK * PASS], rounded[0][:])[2 * b + a]
             weave(nc.scalar.copy, woven, w1_raw[a, b].rearrange("p (j c) -> p j c", j=PACK))
             w1_q[a, b] = quantize(operands[2 * b + a], woven)
 
@@ -312,8 +312,9 @@ def tile_list_gas_well_board_kernel(
         reduce_h1(2, 4)
         make_w1(0, 1)
         make_w1(1, 1)
-        sine(h_slot(2), 2)
-        sine(h_slot(3), 3)
+        late_h = rounded[0][:].bitcast(F32)
+        sine(late_h[:, 0:S], 2)
+        sine(late_h[:, S : 2 * S], 3)
         product_h1(1)
         reduce_h1(0, 2)
         reduce_h1(2, 4)
@@ -322,8 +323,8 @@ def tile_list_gas_well_board_kernel(
             sine(h_slot(4 + t), t)
         fetch(0)
         fetch(1)
-        put_h1(2, h_slot(2))
-        put_h1(3, h_slot(3))
+        put_h1(2, late_h[:, 0:S])
+        put_h1(3, late_h[:, S : 2 * S])
         w3_q = [quantize(operands[a], round_weight(rounded[1 + a], w3_raw[a])) for a in range(2)]
         fetch(2)
         fetch(3)

@@ -52,15 +52,15 @@ def tile_list_gas_well_board_kernel(
             nc.sync.dma_start(tile[:].bitcast(I32), src.rearrange("p c i -> p (c i)").bitcast(I32))
             return tile
 
-        def cleared_scales(name, src):
+        def cleared_scales(name, src, engine):
             tile = kept(name, [P, src.shape[2]], U8)
-            nc.vector.memset(tile[:].bitcast(I32), 0)
+            engine.memset(tile[:].bitcast(I32), 0)
             return tile
 
-        def load_scales(tile, src):
+        def load_scales(tile, src, engine):
             passes = src.shape[0]
             for q in range(QUADS):
-                nc.sync.dma_start(
+                engine.dma_start(
                     tile[32 * q : 32 * q + 4 * passes, :].bitcast(I32),
                     src[:, 4 * q : 4 * q + 4, :].bitcast(I32),
                 )
@@ -131,10 +131,12 @@ def tile_list_gas_well_board_kernel(
             nc.vector.tensor_copy(picked[:], table[:].indirect(offsets[:]))
             return picked
 
-        tab2_s = cleared_scales("tab2_s", tab2_scales)
-        w2_s = cleared_scales("w2_s", w2_scales)
-        tab_s = cleared_scales("tab_s", tab_scales)
-        w4_s = cleared_scales("w4_s", w4_scales)
+        tab2_s = cleared_scales("tab2_s", tab2_scales, nc.vector)
+        w2_s = cleared_scales("w2_s", w2_scales, nc.vector)
+        tab_s = cleared_scales("tab_s", tab_scales, nc.gpsimd)
+        w4_s = cleared_scales("w4_s", w4_scales, nc.gpsimd)
+        load_scales(tab_s, tab_scales, nc.gpsimd)
+        load_scales(w4_s, w4_scales, nc.gpsimd)
         one = kept("one", [P, 1], F32)
         nc.vector.memset(one[:], 1.0)
         quarter_turn = kept("quarter_turn", [P, 1], F32)
@@ -153,8 +155,8 @@ def tile_list_gas_well_board_kernel(
         load_w2(0)
         nc.sync.dma_start(gate_rows[:, 0:S], wg2)
         list4 = load_list("list4", offs4)
-        load_scales(tab2_s, tab2_scales)
-        load_scales(w2_s, w2_scales)
+        load_scales(tab2_s, tab2_scales, nc.sync)
+        load_scales(w2_s, w2_scales, nc.sync)
         load_w2(1)
         load_page(0)
         load_page(1)
@@ -169,7 +171,6 @@ def tile_list_gas_well_board_kernel(
         tab_w = [load_words("tab_w0", tab_words[0])]
         load_page(4)
         tab_w.append(load_words("tab_w1", tab_words[1]))
-        load_scales(tab_s, tab_scales)
         w1_raw = {}
         for a in range(2):
             w1_raw[a, 0] = load_weight(wide[a][:], w1[a * PASS : (a + 1) * PASS, 0:PASS])
@@ -177,7 +178,6 @@ def tile_list_gas_well_board_kernel(
         load_page(6)
         load_page(7)
         w4_w = [load_words("w4_w%d" % a, w4_words[a]) for a in range(2)]
-        load_scales(w4_s, w4_scales)
         w1_raw[0, 1] = load_weight(wide[2][:], w1[0:PASS, PASS:H])
 
         v2_w = gather("v2_w", tab2_w, list2, U32)
@@ -389,21 +389,28 @@ def tile_list_gas_well_board_kernel(
         y_words = out_1[0].rearrange("p m t -> p (m t)").bitcast(I32)
         results = {}
 
+        squares = [[wide[1 + h][:, S * c : S * (c + 1)] for h in range(2)] for c in range(CHUNKS)]
+
         def combine(c):
             damp = picked[c % 3].rearrange("p (t c) -> p t c", t=PACK)
             y = rows_h[1 + c % 3][:].rearrange("p u (v c) -> p (u v) c", v=2)
             for h in range(2):
                 part = slice(2 * h, 2 * h + 2)
-                nc.scalar.activation(damp[:, part, :], accs[c, 1, h][:], ACT.Square)
-                nc.scalar.activation(damp[:, part, :], damp[:, part, :], ACT.Abs_reciprocal_sqrt, bias=one[:])
+                square = squares[c][h].rearrange("p (u j) -> p u j", u=2)
+                nc.scalar.activation(square, accs[c, 1, h][:], ACT.Square)
+                nc.scalar.activation(damp[:, part, :], square, ACT.Abs_reciprocal_sqrt, bias=one[:])
                 nc.vector.tensor_tensor(y[:, part, :], accs[c, 0, h][:], damp[:, part, :], MULT)
             nc.sync.dma_start(y_rows[:, :, CHUNK * c : CHUNK * (c + 1)], y)
             results[c] = y
 
         def hand_out(c):
             cols = slice(CHUNK * c, CHUNK * (c + 1))
-            woven = woven_chunks[c]
-            weave(nc.scalar.copy if c == 2 else nc.vector.tensor_copy, woven, results[c])
+            woven = squares[c + 1][0].bitcast(BF16) if c < 2 else woven_chunks[c]
+            cut = (CHUNK, CHUNK, 0, 160)[c]
+            if cut > 0:
+                weave(nc.vector.tensor_copy, woven[:, 0 : PACK * cut], results[c][:, :, 0:cut])
+            if cut < CHUNK:
+                weave(nc.scalar.copy, woven[:, PACK * cut : PACK * CHUNK], results[c][:, :, cut:CHUNK])
             codes = kept("y_codes%d" % c, [P, CHUNK], U32)
             nc.vector.quantize_mx(
                 out=codes[:].bitcast(FP8X4), scales=y_scales[:, cols], in_=woven
@@ -429,12 +436,12 @@ def tile_list_gas_well_board_kernel(
         hand_out(0)
         first_pass(3)
         second_pass(3)
-        hand_out(1)
         combine(2)
+        hand_out(1)
         combine(3)
         hand_out(2)
         hand_out(3)
         for q in range(QUADS):
-            nc.sync.dma_start(
+            (nc.sync, nc.scalar)[q % 2].dma_start(
                 out_2[0, 4 * q : 4 * q + 4, :].bitcast(I32), y_scales[32 * q : 32 * q + 4, :].bitcast(I32)
             )

import math
from contextlib import ExitStack

import concourse.mybir as mybir
from concourse.masks import make_identity

K, K2, T, TB, S, H, T2, PICKS, N = 1024, 512, 2048, 1024, 512, 1024, 2048, 1024, 512
FLOPS = 2 * (K * H * S + K2 * H * S + 2 * H * N * PICKS)

F32 = mybir.dt.float32
BF16 = mybir.dt.bfloat16
I32 = mybir.dt.int32
U32 = mybir.dt.uint32
U16 = mybir.dt.uint16
U8 = mybir.dt.uint8
FP8X4 = mybir.dt.float8_e4m3fn_x4
FP4X4 = mybir.dt.float4_e2m1fn_x4
ACT = mybir.ActivationFunctionType
MULT = mybir.AluOpType.mult
ADD = mybir.AluOpType.add

P = 128
PACK = 4
PASS = P * PACK
ROW_TILES = H // P
CHUNK = 256
CHUNKS = PICKS // CHUNK
QUADS = 4


def tile_list_gas_well_board_kernel(
    tc, tab_words, tab_scales, tab2_words, tab2_scales, offs, offs2, offs3, offs4, offs5,
    w1, w2_words, w2_scales, wg1, wg2, page0, gain, w3, w4_words, w4_scales, out_0, out_1, out_2,
):
    nc = tc.nc
    with ExitStack() as ctx:
        keep = ctx.enter_context(tc.tile_pool(name="keep", bufs=1))
        psum = ctx.enter_context(tc.psum_pool(name="psum", bufs=1))

        def kept(name, shape, dtype):
            return keep.tile(shape, dtype, name=name, align_bytes=64)

        banks = [psum.tile([P, PASS], F32, name="bank%d" % n) for n in range(8)]

        def load_list(name, src):
            tile = keep.tile(list(src.shape), U16, name=name)
            nc.sync.dma_start(tile[:], src)
            return tile

        def load_words(name, src):
            tile = kept(name, [P, src.shape[1]], U32)
            nc.sync.dma_start(tile[:].bitcast(I32), src.rearrange("p c i -> p (c i)").bitcast(I32))
            return tile

        def cleared_scales(name, src, engine):
            tile = kept(name, [P, src.shape[2]], U8)
            engine.memset(tile[:].bitcast(I32), 0)
            return tile

        def load_scales(tile, src, engine):
            passes = src.shape[0]
            for q in range(QUADS):
                engine.dma_start(
                    tile[32 * q : 32 * q + 4 * passes, :].bitcast(I32),
                    src[:, 4 * q : 4 * q + 4, :].bitcast(I32),
                )

        wide = [kept("wide%d" % n, [P, PACK * PASS], F32) for n in range(3)]
        rounded = [kept("rounded%d" % n, [P, PACK * PASS], BF16) for n in range(3)]
        rows_h = [kept("rows_h%d" % n, [P, 2, S], F32) for n in range(4)]
        fetched = kept("fetched", [P, 3 * PICKS], F32)
        picked = [fetched[:, PICKS * n : PICKS * (n + 1)] for n in range(3)]
        shared = kept("shared", [P, PACK * S], F32)
        gate1 = kept("gate1", [P, PACK * S], F32)
        dist = kept("dist", [P, PACK * S], F32)
        x1_woven = kept("x1_woven", [P, PACK * PICKS], BF16)
        turns = x1_woven[:].bitcast(F32)
        identity = kept("identity", [P, P], F32)
        make_identity(nc, identity[:])
        gate_rows = rounded[2][:].bitcast(F32)

        def turn_gate(rows):
            for n in range(S // P):
                nc.tensor.transpose(banks[7][:, P * n : P * (n + 1)], rows[:, P * n : P * (n + 1)], identity[:])

        def deal_gate(gate, t):
            spread = picked[2][:, 0:S]
            nc.scalar.copy(
                spread.rearrange("p (n a q) -> p n a q", a=QUADS, q=32),
                banks[7][:].rearrange("p (n q t) -> p n t q", q=32, t=PACK)[:, :, t, :]
                .unsqueeze(2).to_broadcast([P, S // P, QUADS, 32]),
            )
            acc = banks[4 + t % 3]
            for n in range(S // P):
                nc.tensor.transpose(acc[:, P * n : P * (n + 1)], spread[:, P * n : P * (n + 1)], identity[:])
            nc.scalar.copy(gate[:, S * t : S * (t + 1)], acc[:])

        pages = {}

        def load_page(i):
            b, t = divmod(i, PACK)
            pages[i] = kept("page%d" % i, [P, T2], F32)
            nc.sync.dma_start(pages[i][:], page0.rearrange("(b p t) c -> b t p c", p=P, t=PACK)[b, t])

        def load_weight(raw, rows):
            nc.sync.dma_start(raw.rearrange("p (j c) -> p j c", j=PACK), rows.rearrange("(p j) c -> p j c", j=PACK))
            return raw

        def round_weight(dealt, raw):
            nc.scalar.copy(
                dealt[:].rearrange("p (t m j) -> p m t j", t=PACK, j=PACK),
                raw.rearrange("p (j m t) -> p m t j", j=PACK, t=PACK),
            )
            return dealt[:]

        def mx_tiles(name, width):
            return kept(name + "_codes", [P, width], U32), kept(name + "_scales", [P, width], U8)

        def quantize(tiles, src):
            codes, scales = tiles
            nc.vector.quantize_mx(out=codes[:].bitcast(FP8X4), scales=scales[:], in_=src)
            return tiles

        def weave(engine_copy, dst, src):
            engine_copy(dst.rearrange("p (c i t) -> p c t i", i=4, t=PACK), src.rearrange("p t (c i) -> p c t i", i=4))

        operands = [mx_tiles("operand%d" % n, PASS) for n in range(4)]

        def gather(name, table, offsets, dtype):
            picked = kept(name, [P, S], dtype)
            nc.vector.tensor_copy(picked[:], table[:].indirect(offsets[:]))
            return picked

        tab2_s = cleared_scales("tab2_s", tab2_scales, nc.vector)
        w2_s = cleared_scales("w2_s", w2_scales, nc.vector)
        tab_s = cleared_scales("tab_s", tab_scales, nc.gpsimd)
        w4_s = cleared_scales("w4_s", w4_scales, nc.gpsimd)
        load_scales(tab_s, tab_scales, nc.gpsimd)
        load_scales(w4_s, w4_scales, nc.gpsimd)
        one = kept("one", [P, 1], F32)
        nc.vector.memset(one[:], 1.0)
        quarter_turn = kept("quarter_turn", [P, 1], F32)
        nc.vector.tensor_scalar(quarter_turn[:], one[:], math.pi / 2, None, MULT)
        minus_quarter_turn = kept("minus_quarter_turn", [P, 1], F32)
        nc.vector.tensor_scalar(minus_quarter_turn[:], one[:], -math.pi / 2, None, MULT)
        warm = kept("warm", [P, 1], F32)
        nc.scalar.activation(warm[:], one[:], ACT.Sin)
        list2 = load_list("list2", offs2)
        tab2_w = load_words("tab2_w", tab2_words[0])
        w2_w = [kept("w2_w%d" % b, [P, 2 * PASS], U8) for b in range(2)]

        def load_w2(b):
            nc.sync.dma_start(w2_w[b][:].bitcast(I32), w2_words[0][:, 2 * PASS * b : 2 * PASS * (b + 1)].bitcast(I32))

        load_w2(0)
        nc.sync.dma_start(gate_rows[:, 0:S], wg2)
        list4 = load_list("list4", offs4)
        load_scales(tab2_s, tab2_scales, nc.sync)
        load_scales(w2_s, w2_scales, nc.sync)
        load_w2(1)
        load_page(0)
        load_page(1)
        load_page(2)
        nc.sync.dma_start(gate_rows[:, S : 2 * S], wg1)
        list1 = load_list("list1", offs)
        list3 = load_list("list3", offs3)
        list5 = load_list("list5", offs5)
        gains = kept("gains", [P, 2, PACK], F32)
        nc.sync.dma_start(gains[:], gain.rearrange("(b p t) -> p b t", p=P, t=PACK))
        load_page(3)
        tab_w = [load_words("tab_w0", tab_words[0])]
        load_page(4)
        tab_w.append(load_words("tab_w1", tab_words[1]))
        w1_raw = {}
        for a in range(2):
            w1_raw[a, 0] = load_weight(wide[a][:], w1[a * PASS : (a + 1) * PASS, 0:PASS])
        load_page(5)
        load_page(6)
        load_page(7)
        w4_w = [load_words("w4_w%d" % a, w4_words[a]) for a in range(2)]
        w1_raw[0, 1] = load_weight(wide[2][:], w1[0:PASS, PASS:H])

        v2_w = gather("v2_w", tab2_w, list2, U32)
        w2_dealt = [kept("w2_dealt%d" % b, [P, 2 * PASS], U8) for b in range(2)]
        w2_s_dealt = [kept("w2_s_dealt%d" % b, [P, PASS], U8) for b in range(2)]

        def deal_w2_words(b):
            nc.vector.tensor_copy(
                w2_dealt[b][:].rearrange("p (t o i e) -> p o t i e", t=PACK, i=8, e=2),
                w2_w[b][:].rearrange("p (o i t e) -> p o t i e", t=PACK, i=8, e=2),
            )

        def deal_scales(dst, src):
            nc.vector.tensor_copy(
                dst.rearrange("p (t o i) -> p o t i", t=PACK, i=16),
                src.rearrange("p (o i t) -> p o t i", t=PACK, i=16),
            )

        deal_w2_words(0)
        v2_s = gather("v2_s", tab2_s, list2, U8)
        deal_scales(w2_s_dealt[0][:], w2_s[:, 0:PASS])
        deal_w2_words(1)
        deal_scales(w2_s_dealt[1][:], w2_s[:, PASS:H])

        def scatter(i, offsets, h, gate):
            nc.vector.tensor_tensor(pages[i][:].indirect(offsets[:]), h, gate, MULT)

        def put_h2(i, h):
            b, t = divmod(i, PACK)
            acc = banks[t]
            nc.tensor.matmul_mx(
                out=acc[:],
                lhsT=w2_dealt[b][:, 2 * P * t : 2 * P * (t + 1)].bitcast(FP4X4),
                lhsT_scale=w2_s_dealt[b][:, P * t : P * (t + 1)],
                rhs=v2_w[:].bitcast(FP8X4), rhs_scale=v2_s[:], start=True, stop=True,
            )
            nc.scalar.activation(h, acc[:], ACT.Abs)
            scatter(i, list4, h, shared[:, S * t : S * (t + 1)])

        turn_gate(gate_rows[:, 0:S])
        for i in range(4):
            deal_gate(shared, i)
            put_h2(i, rows_h[i // 2][:, i % 2, :])
        turn_gate(gate_rows[:, S : 2 * S])
        for t in range(PACK):
            deal_gate(gate1, t)
        v1_w = [gather("v1_w0", tab_w[0], list1, U32)]
        put_h2(4, rows_h[2][:, 0, :])
        v1_w.append(gather("v1_w1", tab_w[1], list1, U32))
        v1_s = gather("v1_s", tab_s, list1, U8)

        w1_q = {}

        def make_w1(a, b):
            woven = (rounded[0][:], rounded[1][:], x1_woven[:, 0 : PACK * PASS], rounded[0][:])[2 * b + a]
            weave(nc.scalar.copy, woven, w1_raw[a, b].rearrange("p (j c) -> p j c", j=PACK))
            w1_q[a, b] = quantize(operands[2 * b + a], woven)

        def product_h1(b):
            for a in range(2):
                codes, scales = w1_q[a, b]
                for n in range(S // P):
                    cols = slice(P * n, P * (n + 1))
                    nc.tensor.matmul_mx(
                        out=banks[n][:], lhsT=v1_w[a][:, cols].bitcast(FP8X4), lhsT_scale=v1_s[4 * a : P, cols],
                        rhs=codes[:].bitcast(FP8X4), rhs_scale=scales[:], start=(a == 0), stop=(a == 1),
                    )
            for n in range(S // P):
                nc.scalar.activation(
                    dist[:, S * n : S * (n + 1)].rearrange("p (t m) -> p t m", t=PACK),
                    banks[n][:].rearrange("p (m t) -> p t m", t=PACK),
                    ACT.Abs, bias=minus_quarter_turn[:],
                )

        def reduce_h1(t0, t1):
            cols = slice(S * t0, S * t1)
            by_tile = dist[:].rearrange("p (n t m) -> p t n m", t=PACK, m=P)
            nc.scalar.activation(
                turns[:, cols].bitcast(U32).rearrange("p (t n m) -> p t n m", n=S // P, m=P), by_tile[:, t0:t1],
                ACT.Copy, scale=1 / (2 * math.pi), bias=-0.25,
            )
            nc.scalar.activation(turns[:, cols], turns[:, cols].bitcast(U32), ACT.Copy, scale=-2 * math.pi)
            for t in range(t0, t1):
                for n in range(S // P):
                    for src, first in ((by_tile[:, t, n], True), (turns[:, S * t + P * n : S * t + P * (n + 1)], False)):
                        nc.tensor.matmul(
                            banks[4 + t][:, P * n : P * (n + 1)], lhsT=src,
                            rhs=identity[:], start=first, stop=not first, is_transpose=True,
                        )

        def sine(out, t):
            nc.scalar.activation(out, banks[4 + t][:], ACT.Sin, scale=-1.0, bias=quarter_turn[:])

        def put_h1(i, h):
            scatter(i, list3, h, gate1[:, S * (i % PACK) : S * (i % PACK + 1)])

        planes = shared[:].bitcast(BF16).rearrange("p (c t j) -> p c t j", c=CHUNKS, t=PACK)

        def fetch(i):
            b, t = divmod(i, PACK)
            nc.vector.tensor_copy(picked[i % 3], pages[i][:].indirect(list5[:]))
            nc.scalar.activation(
                planes[:, :, t, :], picked[i % 3].rearrange("p (c j) -> p c j", c=CHUNKS),
                ACT.Copy, scale=gains[:, b, t : t + 1],
            )

        def h_slot(i):
            return rows_h[i // 2][:, i % 2, :]

        make_w1(0, 0)
        make_w1(1, 0)
        put_h2(5, wide[1][:, 0:S])
        put_h2(6, h_slot(6))
        put_h2(7, h_slot(7))
        product_h1(0)
        w4_dealt = [kept("w4_dealt%d" % a, [P, N], U32) for a in range(2)]
        for a in range(2):
            nc.vector.tensor_copy(
                w4_dealt[a][:].bitcast(I32).rearrange("p (t o i) -> p o t i", t=PACK, i=4),
                w4_w[a][:].bitcast(I32).rearrange("p (o i t) -> p o t i", t=PACK, i=4),
            )
        w4_s_dealt = kept("w4_s_dealt", [P, N], U8)
        deal_scales(w4_s_dealt[:], w4_s[:])
        w1_raw[1, 1] = load_weight(fetched[:, 0 : 2 * PICKS], w1[PASS:K, PASS:H])
        w3_raw = [load_weight(wide[0][:], w3[0:PASS, :])]
        reduce_h1(0, 1)
        reduce_h1(1, 2)
        sine(h_slot(0), 0)
        sine(h_slot(1), 1)
        put_h1(0, h_slot(0))
        put_h1(1, h_slot(1))
        reduce_h1(2, 4)
        make_w1(0, 1)
        make_w1(1, 1)
        late_h = rounded[0][:].bitcast(F32)
        sine(late_h[:, 0:S], 2)
        sine(late_h[:, S : 2 * S], 3)
        product_h1(1)
        reduce_h1(0, 2)
        reduce_h1(2, 4)
        w3_raw.append(load_weight(dist[:], w3[PASS:H, :]))
        for t in range(3):
            sine(h_slot(4 + t), t)
        fetch(0)
        fetch(1)
        put_h1(2, late_h[:, 0:S])
        put_h1(3, late_h[:, S : 2 * S])
        w3_q = [quantize(operands[a], round_weight(rounded[1 + a], w3_raw[a])) for a in range(2)]
        fetch(2)
        fetch(3)
        put_h1(4, h_slot(4))
        put_h1(5, h_slot(5))
        for c in (2, 3, 0, 1):
            weave(nc.scalar.copy, rounded[c // 2][:, PICKS * (c % 2) : PICKS * (c % 2 + 1)], planes[:, c])
        put_h1(6, h_slot(6))
        fetch(4)
        sine(picked[1][:, 0:S], 3)
        nc.scalar.activation(warm[:], picked[1][:, 0:1], ACT.Abs_reciprocal_sqrt, bias=one[:])
        fetch(5)
        x0_q = {1: quantize(operands[3], rounded[1][:])}
        x0_q[0] = quantize(operands[2], rounded[0][:])
        fetch(6)
        put_h1(7, picked[1][:, 0:S])
        woven_chunks = [x1_woven[:, PICKS * c : PICKS * (c + 1)] for c in range(CHUNKS)]
        for c in range(CHUNKS):
            weave(nc.scalar.copy, woven_chunks[c], planes[:, c])

        accs = {}

        def second_stage(c, a, x_codes, x_scales):
            for side in (1, 0):
                for h in range(2):
                    accs[c, side, h] = banks[4 * (c % 2) + 2 * side + h][:].rearrange("p (u j) -> p u j", u=2)
                    for u in range(2):
                        cols = slice(P * (2 * h + u), P * (2 * h + u + 1))
                        if side == 0:
                            codes, scales = w3_q[a][0][:, cols], w3_q[a][1][:, cols]
                        else:
                            codes, scales = w4_dealt[a][:, cols], w4_s_dealt[4 * a : P, cols]
                        nc.tensor.matmul_mx(
                            out=accs[c, side, h][:, u, :], lhsT=codes.bitcast(FP8X4), lhsT_scale=scales,
                            rhs=x_codes.bitcast(FP8X4), rhs_scale=x_scales,
                            start=(a == 0 and u == 0), stop=(a == 1 and u == 1),
                        )

        def first_pass(c):
            codes, scales = x0_q[c // 2]
            cols = slice(CHUNK * (c % 2), CHUNK * (c % 2 + 1))
            second_stage(c, 0, codes[:, cols], scales[:, cols])

        last = [rows_h[0][:, 0, 0:CHUNK]] + [shared[:, S * c : S * c + CHUNK] for c in range(CHUNKS - 1)]

        def fetch_last(c):
            i = ROW_TILES - 1
            nc.vector.tensor_copy(last[c], pages[i][:].indirect(list5[:, 16 * c : 16 * (c + 1)]))

        def scale_last(c):
            nc.vector.tensor_scalar(
                woven_chunks[c].rearrange("p (c t) -> p c t", t=PACK)[:, :, 3],
                last[c], gains[:, 1, 3:4], None, MULT,
            )

        def second_pass(c):
            codes, scales = quantize(mx_tiles("x1_%d" % c, CHUNK), woven_chunks[c])
            second_stage(c, 1, codes[:], scales[:])

        y_scales = kept("y_scales", [P, PICKS], U8)
        y_rows = out_0.rearrange("(p t) j -> p t j", t=PACK)
        y_words = out_1[0].rearrange("p m t -> p (m t)").bitcast(I32)
        results = {}

        squares = [[wide[1 + h][:, S * c : S * (c + 1)] for h in range(2)] for c in range(CHUNKS)]

        def combine(c):
            damp = picked[c % 3].rearrange("p (t c) -> p t c", t=PACK)
            y = rows_h[1 + c % 3][:].rearrange("p u (v c) -> p (u v) c", v=2)
            for h in range(2):
                part = slice(2 * h, 2 * h + 2)
                square = squares[c][h].rearrange("p (u j) -> p u j", u=2)
                nc.scalar.activation(square, accs[c, 1, h][:], ACT.Square)
                nc.scalar.activation(damp[:, part, :], square, ACT.Abs_reciprocal_sqrt, bias=one[:])
                nc.vector.tensor_tensor(y[:, part, :], accs[c, 0, h][:], damp[:, part, :], MULT)
            nc.sync.dma_start(y_rows[:, :, CHUNK * c : CHUNK * (c + 1)], y)
            results[c] = y

        def hand_out(c):
            cols = slice(CHUNK * c, CHUNK * (c + 1))
            woven = squares[c + 1][0].bitcast(BF16) if c < 2 else woven_chunks[c]
            cut = (CHUNK, CHUNK, 0, 160)[c]
            if cut > 0:
                weave(nc.vector.tensor_copy, woven[:, 0 : PACK * cut], results[c][:, :, 0:cut])
            if cut < CHUNK:
                weave(nc.scalar.copy, woven[:, PACK * cut : PACK * CHUNK], results[c][:, :, cut:CHUNK])
            codes = kept("y_codes%d" % c, [P, CHUNK], U32)
            nc.vector.quantize_mx(
                out=codes[:].bitcast(FP8X4), scales=y_scales[:, cols], in_=woven
            )
            nc.sync.dma_start(y_words[:, cols], codes[:].bitcast(I32))

        first_pass(0)
        first_pass(1)
        fetch_last(0)
        scale_last(0)
        fetch_last(1)
        second_pass(0)
        scale_last(1)
        fetch_last(2)
        second_pass(1)
        scale_last(2)
        fetch_last(3)
        scale_last(3)
        combine(0)
        first_pass(2)
        second_pass(2)
        combine(1)
        hand_out(0)
        first_pass(3)
        second_pass(3)
        combine(2)
        hand_out(1)
        combine(3)
        hand_out(2)
        hand_out(3)
        for q in range(QUADS):
            (nc.sync, nc.scalar)[q % 2].dma_start(
                out_2[0, 4 * q : 4 * q + 4, :].bitcast(I32), y_scales[32 * q : 32 * q + 4, :].bitcast(I32)
            )
